import numpy as np
import ml_dtypes


def mxq(x, axis, fmt="e4m3"):
    dtype, down = {"e4m3": (ml_dtypes.float8_e4m3fn, 7), "e5m2": (ml_dtypes.float8_e5m2, 14)}[fmt]
    v = np.moveaxis(np.asarray(x, np.float32).astype(ml_dtypes.bfloat16).astype(np.float64), axis, -1)
    blocks = v.reshape(v.shape[:-1] + (-1, 32))
    amax = np.abs(blocks).max(-1, keepdims=True)
    byte = np.maximum(np.where(amax > 0, np.frexp(amax)[1] - 1 + 127, 0) - down, 1)
    scale = np.exp2(byte - 127.0)
    codes = (blocks / scale).astype(np.float32).astype(dtype).astype(np.float64)
    return np.moveaxis((codes * scale).reshape(v.shape), -1, axis)


WIDE = False


def mx_kscale(k):
    if not WIDE:
        return np.ones(k)
    levels = np.array([10, -10, 5, -5, 0])
    if k % 512:
        return np.exp2(np.random.permutation(np.resize(levels, k // 32))).repeat(32)
    a = np.empty((k // 512, 16))
    for p in range(k // 512):
        a[p, :8] = np.random.permutation(np.resize(levels, 8))
        for g in range(8):
            far = levels[np.abs(levels - a[p, g]) >= 10]
            a[p, g + 8] = far[np.random.randint(len(far))]
    return np.exp2(a.ravel()).repeat(32)


def f64(x):
    return np.asarray(x).astype(np.float64)


def striped(idx):
    return np.tile(idx.reshape(-1, 16).T, (8, 1)).astype(np.uint16)


def unstriped(offs):
    return offs[:16].T.reshape(-1).astype(np.int64)


def striped8(idx):
    return np.concatenate([x.reshape(-1, 16).T for x in idx]).astype(np.uint16)


def runs(offs, k):
    lists = np.stack([offs[16 * r : 16 * r + 16].T.reshape(-1) for r in range(8)]).astype(np.int64)
    return lists[np.arange(k) % 512 // 64]


def pack_weight(w):
    k, n = w.shape
    w = f64(np.asarray(w, np.float32).astype(ml_dtypes.bfloat16)).reshape(k // 32, 32, n)
    amax = np.abs(w).max(1)
    byte = np.clip(np.where(amax > 0, np.frexp(amax)[1] - 1 + 127 - 7, 1), 1, 254)
    scaled = (w * np.exp2(127.0 - byte)[:, None, :]).reshape(k, n).astype(np.float32)
    words = np.ascontiguousarray(scaled.reshape(k // 512, 128, 4, n).transpose(0, 1, 3, 2)).astype(ml_dtypes.float8_e4m3fn).view(np.uint8)
    return words, np.ascontiguousarray(byte.astype(np.uint8).reshape(k // 512, 16, n))


def unpack_weight(words, scales):
    g, p, n, _ = words.shape
    vals = np.ascontiguousarray(words).view(ml_dtypes.float8_e4m3fn).astype(np.float64) * np.repeat(np.exp2(scales.astype(np.float64) - 127.0), 8, axis=1)[..., None]
    return vals.transpose(0, 1, 3, 2).reshape(g * 512, n)


def sigmoid(v):
    return 1.0 / (1.0 + np.exp(-np.maximum(v, -700.0)))


K, T, S, G, H = 512, 2048, 512, 2048, 512


def setup_inputs():
    n = np.random.standard_normal
    s = mx_kscale(K)[:, None]
    packed_xT = pack_weight(n((K, T)) * s)
    packed_dT = pack_weight(n((K, G)) / s)
    return {
        "x_words": packed_xT[0],
        "x_scales": packed_xT[1],
        "d_words": packed_dT[0],
        "d_scales": packed_dT[1],
        "gs": (np.random.uniform(0.5, 1.5, (K, 1)) * s).astype(np.float32),
        "offs": striped(np.random.permutation(T)[:S]),
        "k1": striped8(np.random.randint(0, G, (8, H))),
        "k2": striped8(np.random.randint(0, G, (8, H))),
        "k3": striped8(np.random.randint(0, G, (8, H))),
    }


def reference(x_words, x_scales, d_words, d_scales, gs, offs, k1, k2, k3):
    d_k3 = unpack_weight(d_words, d_scales)[np.arange(K)[:, None], runs(k3, K)]
    d_k1 = unpack_weight(d_words, d_scales)[np.arange(K)[:, None], runs(k1, K)]
    xq = unpack_weight(x_words, x_scales)[:, unstriped(offs)]
    a = 0.0625 * (d_k1.T @ xq)
    d_k2 = unpack_weight(d_words, d_scales)[np.arange(K)[:, None], runs(k2, K)]
    b = sigmoid(0.0625 * (d_k2.T @ xq))
    z = f64(gs) * (a * b)
    return 0.0625 * ((d_k3.T @ mxq(z, 0, "e4m3")))

@@ -1,0 +1,187 @@
+from contextlib import ExitStack
+
+import concourse.mybir as mybir
+
+K, T, S, G, H = 512, 2048, 512, 2048, 512
+FLOPS = 3 * 2 * K * H * S
+
+F32 = mybir.dt.float32
+BF16 = mybir.dt.bfloat16
+I32 = mybir.dt.int32
+U32 = mybir.dt.uint32
+U16 = mybir.dt.uint16
+U8 = mybir.dt.uint8
+FP8X4 = mybir.dt.float8_e4m3fn_x4
+ACT = mybir.ActivationFunctionType
+ALU = mybir.AluOpType
+
+P = 128
+PACK = 4
+CHUNK = 128
+CHUNKS = S // CHUNK
+SIXTEENTH = 0.0625
+
+
+def tile_picked_pqglu2_sigmoid_p_kernel(
+    tc, x_words, x_scales, d_words, d_scales, gs, offs, k1, k2, k3, out
+):
+    nc = tc.nc
+    with ExitStack() as ctx:
+        lists = ctx.enter_context(tc.tile_pool(name="lists", bufs=1))
+        keep = ctx.enter_context(tc.tile_pool(name="keep", bufs=1))
+        early = ctx.enter_context(tc.tile_pool(name="early", bufs=1))
+        late = ctx.enter_context(tc.tile_pool(name="late", bufs=1))
+        psum = ctx.enter_context(tc.psum_pool(name="psum", bufs=1))
+
+        def u8_tile(name, width):
+            return keep.tile([P, width], U8, name=name, align_bytes=64)
+
+        d_scale_table = u8_tile("d_scale_table", G)
+        x_scale_table = u8_tile("x_scale_table", T)
+        k3_placed = u8_tile("k3_placed", S)
+        for zeroed in (d_scale_table, x_scale_table, k3_placed):
+            nc.vector.memset(zeroed[:].bitcast(I32), 0)
+
+        k2_list = lists.tile([P, H // 16], U16, name="k2_list")
+        offs_list = lists.tile([P, S // 16], U16, name="offs_list")
+        k1_list = lists.tile([P, H // 16], U16, name="k1_list")
+        k3_list = lists.tile([P, H // 16], U16, name="k3_list")
+        d_table = keep.tile([P, G], I32, name="d_table", align_bytes=64)
+        x_table = late.tile([P, T], I32, name="x_table", align_bytes=64, offset=0)
+        gs_cols = keep.tile([P, PACK], F32, name="gs_cols")
+
+        nc.sync.dma_start(k2_list[:], k2)
+        nc.scalar.dma_start(d_scale_table[0:P:8, :].bitcast(I32), d_scales[0].bitcast(I32))
+        nc.sync.dma_start(k1_list[:], k1)
+        nc.sync.dma_start(offs_list[:], offs)
+        nc.scalar.dma_start(x_scale_table[0:P:8, :].bitcast(I32), x_scales[0].bitcast(I32))
+        nc.sync.dma_start(k3_list[:], k3)
+        nc.sync.dma_start(d_table[:], d_words[0].rearrange("p n t -> p (n t)").bitcast(I32))
+        nc.sync.dma_start(x_table[:], x_words[0].rearrange("p n t -> p (n t)").bitcast(I32))
+        nc.gpsimd.dma_start(gs_cols[:], gs.rearrange("(p t) o -> p (t o)", t=PACK))
+
+        gs16 = keep.tile([P, PACK], F32, name="gs16")
+        nc.gpsimd.tensor_scalar(gs16[:], gs_cols[:], SIXTEENTH, 0.0, ALU.mult, ALU.add)
+
+        def place(placed, picked):
+            for c in range(4):
+                nc.sync.dma_start(placed[c:P:32, :].bitcast(I32), picked[8 * c : P : 32, :].bitcast(I32))
+
+        def deal(dealt, picked):
+            nc.vector.tensor_copy(
+                dealt.rearrange("p (t m) -> p m t", t=PACK), picked.rearrange("p (m t) -> p m t", t=PACK)
+            )
+
+        first_picked = early.tile([P, 3 * S], U8, name="first_picked", align_bytes=64, offset=1280)
+        nc.vector.tensor_copy(first_picked[:, 0:S], d_scale_table[:].indirect(k2_list[:]))
+        nc.vector.tensor_copy(first_picked[:, S : 2 * S], d_scale_table[:].indirect(k1_list[:]))
+        nc.vector.tensor_copy(first_picked[:, 2 * S : 3 * S], x_scale_table[:].indirect(offs_list[:]))
+        first_placed = u8_tile("first_placed", 3 * S)
+        nc.vector.tensor_copy(
+            first_placed[:, 0 : 2 * S].rearrange("p (l t m) -> p l m t", l=2, t=PACK),
+            first_picked[:, 0 : 2 * S].rearrange("p (l m t) -> p l m t", l=2, t=PACK),
+        )
+        nc.vector.tensor_copy(
+            first_placed[:, 2 * S : 3 * S].bitcast(I32), first_picked[:, 2 * S : 3 * S].bitcast(I32)
+        )
+        for c, queue in ((1, nc.sync), (2, nc.scalar), (3, nc.sync)):
+            queue.dma_start(first_placed[c:P:32, :].bitcast(I32), first_placed[8 * c : P : 32, :].bitcast(I32))
+        k2_scale = first_placed[:, 0:S]
+        k1_scale = first_placed[:, S : 2 * S]
+        x_scale = first_placed[:, 2 * S : 3 * S]
+
+        def late_tile(name, dtype, offset):
+            return late.tile([P, S], dtype, name=name, align_bytes=64, offset=offset)
+
+        k2_picked = early.tile([P, H], U32, name="k2_picked", align_bytes=64, offset=0)
+        x_codes = early.tile([P, S], U32, name="x_codes", align_bytes=64, offset=2048)
+        nc.vector.tensor_copy(k2_picked[:], d_table[:].bitcast(U32).indirect(k2_list[:]))
+        nc.vector.tensor_copy(x_codes[:], x_table[:].bitcast(U32).indirect(offs_list[:]))
+
+        k2_codes = late_tile("k2_codes", U32, 0)
+        k1_picked = late_tile("k1_picked", U32, 2048)
+        k1_codes = late_tile("k1_codes", U32, 4096)
+        k3_scale_picked = late_tile("k3_scale_picked", U8, 7168)
+
+        deal(k2_codes[:], k2_picked[:])
+
+        def product(bank, codes, scale, rhs, rhs_scale, blocks=range(PACK)):
+            for slot, t in enumerate(blocks):
+                cols = slice(P * t, P * (t + 1))
+                nc.tensor.matmul_mx(
+                    bank[:, slot, :],
+                    lhsT=codes[:, cols].bitcast(FP8X4),
+                    lhsT_scale=scale[:, cols],
+                    rhs=rhs.bitcast(FP8X4),
+                    rhs_scale=rhs_scale,
+                    start=True,
+                    stop=True,
+                )
+
+        def tokens(c):
+            return slice(CHUNK * c, CHUNK * (c + 1))
+
+        gates = []
+        for c in range(CHUNKS):
+            b_bank = psum.tile([P, PACK, CHUNK], F32, name="b_bank%d" % c, tag="gate_then_out%d" % c)
+            product(b_bank, k2_codes, k2_scale, x_codes[:, tokens(c)], x_scale[:, tokens(c)])
+            sig = keep.tile([P, PACK, CHUNK], F32, name="sig%d" % c)
+            nc.scalar.activation(sig[:], b_bank[:], ACT.Sigmoid, scale=SIXTEENTH)
+            gate = keep.tile([P, PACK, CHUNK], F32, name="gate%d" % c)
+            for t in range(PACK):
+                nc.scalar.activation(gate[:, t, :], sig[:, t, :], ACT.Copy, scale=gs16[:, t : t + 1])
+            gates.append(gate)
+
+        nc.vector.tensor_copy(k1_picked[:], d_table[:].bitcast(U32).indirect(k1_list[:]))
+        nc.vector.tensor_copy(k3_scale_picked[:], d_scale_table[:].indirect(k3_list[:]))
+        place(k3_placed, k3_scale_picked)
+        deal(k1_codes[:], k1_picked[:])
+        k3_codes = late_tile("k3_codes", U32, 2048)
+        nc.vector.tensor_copy(k3_codes[:], d_table[:].bitcast(U32).indirect(k3_list[:]))
+
+        a_banks = []
+        for c in range(CHUNKS):
+            a_bank = psum.tile([P, PACK, CHUNK], F32, name="a_bank%d" % c, tag="a_bank%d" % c)
+            product(a_bank, k1_codes, k1_scale, x_codes[:, tokens(c)], x_scale[:, tokens(c)])
+            a_banks.append(a_bank)
+
+        out_rows = out.rearrange("(o m) n -> m o n", m=P)
+
+        def gated(c):
+            z = keep.tile([P, CHUNK, PACK], BF16, name="z%d" % c, align_bytes=64)
+            nc.vector.tensor_tensor(
+                z[:].rearrange("p (g i) t -> p g t i", i=4),
+                a_banks[c][:].rearrange("p t (g i) -> p g t i", i=4),
+                gates[c][:].rearrange("p t (g i) -> p g t i", i=4),
+                ALU.mult,
+            )
+            return z
+
+        def quantised(c, z):
+            z_codes = keep.tile([P, CHUNK], U32, name="z_codes%d" % c, align_bytes=64)
+            z_scale = keep.tile([P, CHUNK], U8, name="z_scale%d" % c, align_bytes=64)
+            nc.vector.quantize_mx(z_codes[:].bitcast(FP8X4), z_scale[:], z[:].rearrange("p n t -> p (n t)"))
+            return z_codes, z_scale
+
+        def finish(c, zq, blocks, tag, on_scalar):
+            name = "%d_%d" % (c, blocks.start)
+            out_bank = psum.tile([P, len(blocks), CHUNK], F32, name="out_bank" + name, tag=tag)
+            product(out_bank, k3_codes, k3_placed, zq[0][:], zq[1][:], blocks)
+            result = keep.tile([P, len(blocks), CHUNK], F32, name="result" + name)
+            if on_scalar:
+                nc.scalar.activation(result[:], out_bank[:], ACT.Copy, scale=SIXTEENTH)
+            else:
+                nc.vector.tensor_scalar(result[:], out_bank[:], SIXTEENTH, None, ALU.mult)
+            nc.sync.dma_start(out_rows[:, blocks.start : blocks.stop, tokens(c)], result[:])
+
+        z0 = gated(0)
+        z1 = gated(1)
+        finish(0, quantised(0, z0), range(4), "gate_then_out0", True)
+        z2 = gated(2)
+        finish(1, quantised(1, z1), range(4), "gate_then_out1", True)
+        z3 = gated(3)
+        zq2 = quantised(2, z2)
+        zq3 = quantised(3, z3)
+        finish(2, zq2, range(4), "gate_then_out2", False)
+        finish(3, zq3, range(0, 2), "gate_then_out3", True)
+        finish(3, zq3, range(2, 4), "a_bank0", False)

@@ -20,6 +20,7 @@ PACK = 4
 CHUNK = 128
 CHUNKS = S // CHUNK
 SIXTEENTH = 0.0625
+X_FIRST = 1792
 
 
 def tile_picked_pqglu2_sigmoid_p_kernel(
@@ -29,7 +30,6 @@ def tile_picked_pqglu2_sigmoid_p_kernel(
     with ExitStack() as ctx:
         lists = ctx.enter_context(tc.tile_pool(name="lists", bufs=1))
         keep = ctx.enter_context(tc.tile_pool(name="keep", bufs=1))
-        early = ctx.enter_context(tc.tile_pool(name="early", bufs=1))
         late = ctx.enter_context(tc.tile_pool(name="late", bufs=1))
         psum = ctx.enter_context(tc.psum_pool(name="psum", bufs=1))
 
@@ -38,8 +38,9 @@ def tile_picked_pqglu2_sigmoid_p_kernel(
 
         d_scale_table = u8_tile("d_scale_table", G)
         x_scale_table = u8_tile("x_scale_table", T)
+        first_placed = u8_tile("first_placed", 3 * S)
         k3_placed = u8_tile("k3_placed", S)
-        for zeroed in (d_scale_table, x_scale_table, k3_placed):
+        for zeroed in (d_scale_table, x_scale_table, first_placed, k3_placed):
             nc.vector.memset(zeroed[:].bitcast(I32), 0)
 
         k2_list = lists.tile([P, H // 16], U16, name="k2_list")
@@ -51,41 +52,43 @@ def tile_picked_pqglu2_sigmoid_p_kernel(
         gs_cols = keep.tile([P, PACK], F32, name="gs_cols")
 
         nc.sync.dma_start(k2_list[:], k2)
-        nc.scalar.dma_start(d_scale_table[0:P:8, :].bitcast(I32), d_scales[0].bitcast(I32))
         nc.sync.dma_start(k1_list[:], k1)
         nc.sync.dma_start(offs_list[:], offs)
-        nc.scalar.dma_start(x_scale_table[0:P:8, :].bitcast(I32), x_scales[0].bitcast(I32))
         nc.sync.dma_start(k3_list[:], k3)
+        nc.sync.dma_start(d_scale_table[0:P:8, :].bitcast(I32), d_scales[0].bitcast(I32))
+        nc.sync.dma_start(x_scale_table[0:P:8, :].bitcast(I32), x_scales[0].bitcast(I32))
+        x_rows = x_words[0].rearrange("p n t -> p (n t)").bitcast(I32)
+        nc.sync.dma_start(x_table[:, 0:X_FIRST], x_rows[:, 0:X_FIRST])
         nc.sync.dma_start(d_table[:], d_words[0].rearrange("p n t -> p (n t)").bitcast(I32))
-        nc.sync.dma_start(x_table[:], x_words[0].rearrange("p n t -> p (n t)").bitcast(I32))
+        nc.sync.dma_start(x_table[:, X_FIRST:T], x_rows[:, X_FIRST:T])
         nc.gpsimd.dma_start(gs_cols[:], gs.rearrange("(p t) o -> p (t o)", t=PACK))
 
         gs16 = keep.tile([P, PACK], F32, name="gs16")
         nc.gpsimd.tensor_scalar(gs16[:], gs_cols[:], SIXTEENTH, 0.0, ALU.mult, ALU.add)
 
-        def place(placed, picked):
+        def place(placed, picked, queues):
             for c in range(4):
-                nc.sync.dma_start(placed[c:P:32, :].bitcast(I32), picked[8 * c : P : 32, :].bitcast(I32))
+                queues[c % len(queues)].dma_start(placed[c:P:32, :].bitcast(I32), picked[8 * c : P : 32, :].bitcast(I32))
 
         def deal(dealt, picked):
             nc.vector.tensor_copy(
-                dealt.rearrange("p (t m) -> p m t", t=PACK), picked.rearrange("p (m t) -> p m t", t=PACK)
+                dealt.rearrange("p (t g i) -> p g t i", t=PACK, i=4),
+                picked.rearrange("p (g i t) -> p g t i", t=PACK, i=4),
             )
 
-        first_picked = early.tile([P, 3 * S], U8, name="first_picked", align_bytes=64, offset=1280)
+        first_picked = u8_tile("first_picked", 3 * S)
         nc.vector.tensor_copy(first_picked[:, 0:S], d_scale_table[:].indirect(k2_list[:]))
         nc.vector.tensor_copy(first_picked[:, S : 2 * S], d_scale_table[:].indirect(k1_list[:]))
         nc.vector.tensor_copy(first_picked[:, 2 * S : 3 * S], x_scale_table[:].indirect(offs_list[:]))
-        first_placed = u8_tile("first_placed", 3 * S)
+        first_dealt = u8_tile("first_dealt", 3 * S)
         nc.vector.tensor_copy(
-            first_placed[:, 0 : 2 * S].rearrange("p (l t m) -> p l m t", l=2, t=PACK),
-            first_picked[:, 0 : 2 * S].rearrange("p (l m t) -> p l m t", l=2, t=PACK),
+            first_dealt[:, 0 : 2 * S].rearrange("p (l t g i) -> p l g t i", l=2, t=PACK, i=16),
+            first_picked[:, 0 : 2 * S].rearrange("p (l g i t) -> p l g t i", l=2, t=PACK, i=16),
         )
         nc.vector.tensor_copy(
-            first_placed[:, 2 * S : 3 * S].bitcast(I32), first_picked[:, 2 * S : 3 * S].bitcast(I32)
+            first_dealt[:, 2 * S : 3 * S].bitcast(I32), first_picked[:, 2 * S : 3 * S].bitcast(I32)
         )
-        for c, queue in ((1, nc.sync), (2, nc.scalar), (3, nc.sync)):
-            queue.dma_start(first_placed[c:P:32, :].bitcast(I32), first_placed[8 * c : P : 32, :].bitcast(I32))
+        place(first_placed, first_dealt, (nc.sync, nc.scalar))
         k2_scale = first_placed[:, 0:S]
         k1_scale = first_placed[:, S : 2 * S]
         x_scale = first_placed[:, 2 * S : 3 * S]
@@ -93,12 +96,12 @@ def tile_picked_pqglu2_sigmoid_p_kernel(
         def late_tile(name, dtype, offset):
             return late.tile([P, S], dtype, name=name, align_bytes=64, offset=offset)
 
-        k2_picked = early.tile([P, H], U32, name="k2_picked", align_bytes=64, offset=0)
-        x_codes = early.tile([P, S], U32, name="x_codes", align_bytes=64, offset=2048)
+        k2_picked = keep.tile([P, H], U32, name="k2_picked", align_bytes=64)
+        x_codes = keep.tile([P, S], U32, name="x_codes", align_bytes=64)
         nc.vector.tensor_copy(k2_picked[:], d_table[:].bitcast(U32).indirect(k2_list[:]))
         nc.vector.tensor_copy(x_codes[:], x_table[:].bitcast(U32).indirect(offs_list[:]))
 
-        k2_codes = late_tile("k2_codes", U32, 0)
+        k2_codes = keep.tile([P, H], U32, name="k2_codes", align_bytes=64)
         k1_picked = late_tile("k1_picked", U32, 2048)
         k1_codes = late_tile("k1_codes", U32, 4096)
         k3_scale_picked = late_tile("k3_scale_picked", U8, 7168)
@@ -134,9 +137,9 @@ def tile_picked_pqglu2_sigmoid_p_kernel(
 
         nc.vector.tensor_copy(k1_picked[:], d_table[:].bitcast(U32).indirect(k1_list[:]))
         nc.vector.tensor_copy(k3_scale_picked[:], d_scale_table[:].indirect(k3_list[:]))
-        place(k3_placed, k3_scale_picked)
+        place(k3_placed, k3_scale_picked, (nc.sync,))
         deal(k1_codes[:], k1_picked[:])
-        k3_codes = late_tile("k3_codes", U32, 2048)
+        k3_codes = late_tile("k3_codes", U32, 0)
         nc.vector.tensor_copy(k3_codes[:], d_table[:].bitcast(U32).indirect(k3_list[:]))
 
         a_banks = []
@@ -163,7 +166,7 @@ def tile_picked_pqglu2_sigmoid_p_kernel(
             nc.vector.quantize_mx(z_codes[:].bitcast(FP8X4), z_scale[:], z[:].rearrange("p n t -> p (n t)"))
             return z_codes, z_scale
 
-        def finish(c, zq, blocks, tag, on_scalar):
+        def finish(c, zq, blocks, tag, on_scalar, queue=nc.sync):
             name = "%d_%d" % (c, blocks.start)
             out_bank = psum.tile([P, len(blocks), CHUNK], F32, name="out_bank" + name, tag=tag)
             product(out_bank, k3_codes, k3_placed, zq[0][:], zq[1][:], blocks)
@@ -172,7 +175,7 @@ def tile_picked_pqglu2_sigmoid_p_kernel(
                 nc.scalar.activation(result[:], out_bank[:], ACT.Copy, scale=SIXTEENTH)
             else:
                 nc.vector.tensor_scalar(result[:], out_bank[:], SIXTEENTH, None, ALU.mult)
-            nc.sync.dma_start(out_rows[:, blocks.start : blocks.stop, tokens(c)], result[:])
+            queue.dma_start(out_rows[:, blocks.start : blocks.stop, tokens(c)], result[:])
 
         z0 = gated(0)
         z1 = gated(1)
@@ -182,6 +185,7 @@ def tile_picked_pqglu2_sigmoid_p_kernel(
         z3 = gated(3)
         zq2 = quantised(2, z2)
         zq3 = quantised(3, z3)
-        finish(2, zq2, range(4), "gate_then_out2", False)
-        finish(3, zq3, range(0, 2), "gate_then_out3", True)
+        finish(2, zq2, range(0, 2), "gate_then_out2", True)
+        finish(2, zq2, range(2, 4), "a_bank1", False)
+        finish(3, zq3, range(0, 2), "gate_then_out3", True, nc.scalar)
         finish(3, zq3, range(2, 4), "a_bank0", False)

from contextlib import ExitStack

import concourse.mybir as mybir

K, T, S, G, H = 512, 2048, 512, 2048, 512
FLOPS = 3 * 2 * K * H * S

F32 = mybir.dt.float32
BF16 = mybir.dt.bfloat16
I32 = mybir.dt.int32
U32 = mybir.dt.uint32
U16 = mybir.dt.uint16
U8 = mybir.dt.uint8
FP8X4 = mybir.dt.float8_e4m3fn_x4
ACT = mybir.ActivationFunctionType
ALU = mybir.AluOpType

P = 128
PACK = 4
CHUNK = 128
CHUNKS = S // CHUNK
SIXTEENTH = 0.0625
X_FIRST = 1792


def tile_picked_pqglu2_sigmoid_p_kernel(
    tc, x_words, x_scales, d_words, d_scales, gs, offs, k1, k2, k3, out
):
    nc = tc.nc
    with ExitStack() as ctx:
        lists = ctx.enter_context(tc.tile_pool(name="lists", bufs=1))
        keep = ctx.enter_context(tc.tile_pool(name="keep", bufs=1))
        late = ctx.enter_context(tc.tile_pool(name="late", bufs=1))
        psum = ctx.enter_context(tc.psum_pool(name="psum", bufs=1))

        def u8_tile(name, width):
            return keep.tile([P, width], U8, name=name, align_bytes=64)

        d_scale_table = u8_tile("d_scale_table", G)
        x_scale_table = u8_tile("x_scale_table", T)
        first_placed = u8_tile("first_placed", 3 * S)
        k3_placed = u8_tile("k3_placed", S)
        for zeroed in (d_scale_table, x_scale_table, first_placed, k3_placed):
            nc.vector.memset(zeroed[:].bitcast(I32), 0)

        k2_list = lists.tile([P, H // 16], U16, name="k2_list")
        offs_list = lists.tile([P, S // 16], U16, name="offs_list")
        k1_list = lists.tile([P, H // 16], U16, name="k1_list")
        k3_list = lists.tile([P, H // 16], U16, name="k3_list")
        d_table = keep.tile([P, G], I32, name="d_table", align_bytes=64)
        x_table = late.tile([P, T], I32, name="x_table", align_bytes=64, offset=0)
        gs_cols = keep.tile([P, PACK], F32, name="gs_cols")

        nc.sync.dma_start(k2_list[:], k2)
        nc.sync.dma_start(k1_list[:], k1)
        nc.sync.dma_start(offs_list[:], offs)
        nc.sync.dma_start(k3_list[:], k3)
        nc.sync.dma_start(d_scale_table[0:P:8, :].bitcast(I32), d_scales[0].bitcast(I32))
        nc.sync.dma_start(x_scale_table[0:P:8, :].bitcast(I32), x_scales[0].bitcast(I32))
        x_rows = x_words[0].rearrange("p n t -> p (n t)").bitcast(I32)
        nc.sync.dma_start(x_table[:, 0:X_FIRST], x_rows[:, 0:X_FIRST])
        nc.sync.dma_start(d_table[:], d_words[0].rearrange("p n t -> p (n t)").bitcast(I32))
        nc.sync.dma_start(x_table[:, X_FIRST:T], x_rows[:, X_FIRST:T])
        nc.gpsimd.dma_start(gs_cols[:], gs.rearrange("(p t) o -> p (t o)", t=PACK))

        gs16 = keep.tile([P, PACK], F32, name="gs16")
        nc.gpsimd.tensor_scalar(gs16[:], gs_cols[:], SIXTEENTH, 0.0, ALU.mult, ALU.add)

        def place(placed, picked, queues):
            for c in range(4):
                queues[c % len(queues)].dma_start(placed[c:P:32, :].bitcast(I32), picked[8 * c : P : 32, :].bitcast(I32))

        def deal(dealt, picked):
            nc.vector.tensor_copy(
                dealt.rearrange("p (t g i) -> p g t i", t=PACK, i=4),
                picked.rearrange("p (g i t) -> p g t i", t=PACK, i=4),
            )

        first_picked = u8_tile("first_picked", 3 * S)
        nc.vector.tensor_copy(first_picked[:, 0:S], d_scale_table[:].indirect(k2_list[:]))
        nc.vector.tensor_copy(first_picked[:, S : 2 * S], d_scale_table[:].indirect(k1_list[:]))
        nc.vector.tensor_copy(first_picked[:, 2 * S : 3 * S], x_scale_table[:].indirect(offs_list[:]))
        first_dealt = u8_tile("first_dealt", 3 * S)
        nc.vector.tensor_copy(
            first_dealt[:, 0 : 2 * S].rearrange("p (l t g i) -> p l g t i", l=2, t=PACK, i=16),
            first_picked[:, 0 : 2 * S].rearrange("p (l g i t) -> p l g t i", l=2, t=PACK, i=16),
        )
        nc.vector.tensor_copy(
            first_dealt[:, 2 * S : 3 * S].bitcast(I32), first_picked[:, 2 * S : 3 * S].bitcast(I32)
        )
        place(first_placed, first_dealt, (nc.sync, nc.scalar))
        k2_scale = first_placed[:, 0:S]
        k1_scale = first_placed[:, S : 2 * S]
        x_scale = first_placed[:, 2 * S : 3 * S]

        def late_tile(name, dtype, offset):
            return late.tile([P, S], dtype, name=name, align_bytes=64, offset=offset)

        k2_picked = keep.tile([P, H], U32, name="k2_picked", align_bytes=64)
        x_codes = keep.tile([P, S], U32, name="x_codes", align_bytes=64)
        nc.vector.tensor_copy(k2_picked[:], d_table[:].bitcast(U32).indirect(k2_list[:]))
        nc.vector.tensor_copy(x_codes[:], x_table[:].bitcast(U32).indirect(offs_list[:]))

        k2_codes = keep.tile([P, H], U32, name="k2_codes", align_bytes=64)
        k1_picked = late_tile("k1_picked", U32, 2048)
        k1_codes = late_tile("k1_codes", U32, 4096)
        k3_scale_picked = late_tile("k3_scale_picked", U8, 7168)

        deal(k2_codes[:], k2_picked[:])

        def product(bank, codes, scale, rhs, rhs_scale, blocks=range(PACK)):
            for slot, t in enumerate(blocks):
                cols = slice(P * t, P * (t + 1))
                nc.tensor.matmul_mx(
                    bank[:, slot, :],
                    lhsT=codes[:, cols].bitcast(FP8X4),
                    lhsT_scale=scale[:, cols],
                    rhs=rhs.bitcast(FP8X4),
                    rhs_scale=rhs_scale,
                    start=True,
                    stop=True,
                )

        def tokens(c):
            return slice(CHUNK * c, CHUNK * (c + 1))

        gates = []
        for c in range(CHUNKS):
            b_bank = psum.tile([P, PACK, CHUNK], F32, name="b_bank%d" % c, tag="gate_then_out%d" % c)
            product(b_bank, k2_codes, k2_scale, x_codes[:, tokens(c)], x_scale[:, tokens(c)])
            sig = keep.tile([P, PACK, CHUNK], F32, name="sig%d" % c)
            nc.scalar.activation(sig[:], b_bank[:], ACT.Sigmoid, scale=SIXTEENTH)
            gate = keep.tile([P, PACK, CHUNK], F32, name="gate%d" % c)
            for t in range(PACK):
                nc.scalar.activation(gate[:, t, :], sig[:, t, :], ACT.Copy, scale=gs16[:, t : t + 1])
            gates.append(gate)

        nc.vector.tensor_copy(k1_picked[:], d_table[:].bitcast(U32).indirect(k1_list[:]))
        nc.vector.tensor_copy(k3_scale_picked[:], d_scale_table[:].indirect(k3_list[:]))
        place(k3_placed, k3_scale_picked, (nc.sync,))
        deal(k1_codes[:], k1_picked[:])
        k3_codes = late_tile("k3_codes", U32, 0)
        nc.vector.tensor_copy(k3_codes[:], d_table[:].bitcast(U32).indirect(k3_list[:]))

        a_banks = []
        for c in range(CHUNKS):
            a_bank = psum.tile([P, PACK, CHUNK], F32, name="a_bank%d" % c, tag="a_bank%d" % c)
            product(a_bank, k1_codes, k1_scale, x_codes[:, tokens(c)], x_scale[:, tokens(c)])
            a_banks.append(a_bank)

        out_rows = out.rearrange("(o m) n -> m o n", m=P)

        def gated(c):
            z = keep.tile([P, CHUNK, PACK], BF16, name="z%d" % c, align_bytes=64)
            nc.vector.tensor_tensor(
                z[:].rearrange("p (g i) t -> p g t i", i=4),
                a_banks[c][:].rearrange("p t (g i) -> p g t i", i=4),
                gates[c][:].rearrange("p t (g i) -> p g t i", i=4),
                ALU.mult,
            )
            return z

        def quantised(c, z):
            z_codes = keep.tile([P, CHUNK], U32, name="z_codes%d" % c, align_bytes=64)
            z_scale = keep.tile([P, CHUNK], U8, name="z_scale%d" % c, align_bytes=64)
            nc.vector.quantize_mx(z_codes[:].bitcast(FP8X4), z_scale[:], z[:].rearrange("p n t -> p (n t)"))
            return z_codes, z_scale

        def finish(c, zq, blocks, tag, on_scalar, queue=nc.sync):
            name = "%d_%d" % (c, blocks.start)
            out_bank = psum.tile([P, len(blocks), CHUNK], F32, name="out_bank" + name, tag=tag)
            product(out_bank, k3_codes, k3_placed, zq[0][:], zq[1][:], blocks)
            result = keep.tile([P, len(blocks), CHUNK], F32, name="result" + name)
            if on_scalar:
                nc.scalar.activation(result[:], out_bank[:], ACT.Copy, scale=SIXTEENTH)
            else:
                nc.vector.tensor_scalar(result[:], out_bank[:], SIXTEENTH, None, ALU.mult)
            queue.dma_start(out_rows[:, blocks.start : blocks.stop, tokens(c)], result[:])

        z0 = gated(0)
        z1 = gated(1)
        finish(0, quantised(0, z0), range(4), "gate_then_out0", True)
        z2 = gated(2)
        finish(1, quantised(1, z1), range(4), "gate_then_out1", True)
        z3 = gated(3)
        zq2 = quantised(2, z2)
        zq3 = quantised(3, z3)
        finish(2, zq2, range(0, 2), "gate_then_out2", True)
        finish(2, zq2, range(2, 4), "a_bank1", False)
        finish(3, zq3, range(0, 2), "gate_then_out3", True, nc.scalar)
        finish(3, zq3, range(2, 4), "a_bank0", False)
